import numpy as np
import ml_dtypes


def mxq(x, axis, fmt="e4m3"):
    dtype, down = {"e4m3": (ml_dtypes.float8_e4m3fn, 7), "e5m2": (ml_dtypes.float8_e5m2, 14)}[fmt]
    v = np.moveaxis(np.asarray(x, np.float32).astype(ml_dtypes.bfloat16).astype(np.float64), axis, -1)
    blocks = v.reshape(v.shape[:-1] + (-1, 32))
    amax = np.abs(blocks).max(-1, keepdims=True)
    byte = np.maximum(np.where(amax > 0, np.frexp(amax)[1] - 1 + 127, 0) - down, 1)
    scale = np.exp2(byte - 127.0)
    codes = (blocks / scale).astype(np.float32).astype(dtype).astype(np.float64)
    return np.moveaxis((codes * scale).reshape(v.shape), -1, axis)


WIDE = False


def mx_kscale(k):
    if not WIDE:
        return np.ones(k)
    levels = np.array([10, -10, 5, -5, 0])
    if k % 512:
        return np.exp2(np.random.permutation(np.resize(levels, k // 32))).repeat(32)
    a = np.empty((k // 512, 16))
    for p in range(k // 512):
        a[p, :8] = np.random.permutation(np.resize(levels, 8))
        for g in range(8):
            far = levels[np.abs(levels - a[p, g]) >= 10]
            a[p, g + 8] = far[np.random.randint(len(far))]
    return np.exp2(a.ravel()).repeat(32)


BF16 = ml_dtypes.bfloat16


def bf(x):
    return np.asarray(x, np.float32).astype(BF16)


def f64(x):
    return np.asarray(x).astype(np.float64)

def planes(Y):
    n, m = Y.shape
    b = f64(bf(Y)).reshape(n // 32, 32, m)
    amax = np.abs(b).max(1)
    byte = np.clip(np.where(amax > 0, np.frexp(amax)[1] - 1 + 127 - 7, 1), 1, 254)
    codes = (b * np.exp2(127.0 - byte)[:, None, :]).reshape(n, m).astype(np.float32).astype(ml_dtypes.float8_e4m3fn).view(np.uint8)
    words = codes.reshape(n // 512, 128, 4, m).transpose(0, 1, 3, 2)
    return np.ascontiguousarray(words), np.ascontiguousarray(byte.astype(np.uint8).reshape(n // 512, 16, m))


EDGES, NODES, DE, DM = 2048, 1024, 512, 1536

GAIN_SPREAD, WEIGHT_SPREAD, BIAS_SIZE = 0.8, 0.4, 0.3


def setup_inputs():
    randn = np.random.randn
    s = mx_kscale(DE)
    t = mx_kscale(EDGES)
    edge_feats = randn(EDGES, DE) * s[None, :]
    w_msg = randn(DE, DM) / np.sqrt(DE) / s[:, None]
    edge_weight = np.exp(WEIGHT_SPREAD * randn(EDGES)) * t
    incidence = randn(NODES, EDGES) / np.sqrt(EDGES) / t[None, :]
    bias = BIAS_SIZE * randn(DM)
    gain = np.exp(GAIN_SPREAD * randn(DM))
    return {"edge_feats": bf(edge_feats), "w_msg": bf(w_msg), "edge_weight": bf(edge_weight),
            "incidence": bf(incidence), "bias": bf(bias), "gain": bf(gain)}


def reference(edge_feats, w_msg, edge_weight, incidence, bias, gain):
    pre = mxq(f64(edge_feats), 1, "e4m3") @ mxq(f64(w_msg), 0, "e4m3")
    msg = np.tanh(pre) * f64(edge_weight)[:, None]
    agg = mxq(f64(incidence), 1, "e4m3") @ mxq(msg, 0, "e4m3")
    y = (agg + f64(bias)[None, :]) * f64(gain)[None, :]
    Y = y.T
    words, scales = planes(Y)
    return y, words, scales

@@ -1,0 +1,263 @@
+from contextlib import ExitStack
+
+import concourse.mybir as mybir
+from concourse.masks import make_identity
+
+EDGES, NODES, DE, DM = 2048, 1024, 512, 1536
+FLOPS = 2 * EDGES * DE * DM + 2 * NODES * EDGES * DM
+
+F32 = mybir.dt.float32
+BF16 = mybir.dt.bfloat16
+U32 = mybir.dt.uint32
+I32 = mybir.dt.int32
+U8 = mybir.dt.uint8
+FP8X4 = mybir.dt.float8_e4m3fn_x4
+ACT = mybir.ActivationFunctionType
+ALU = mybir.AluOpType
+
+P = 128
+K = 512
+EG = EDGES // K
+DG = DM // K
+NT = NODES // P
+
+SEQ = "W00 X0 X1 W01 H000 X2 H010 X3 H020 I0 H030 I1 H001 W10 I2 H011 I3 H021 W11 I4 H031 I5 H100 S000 I6 H110 S001 I7 H120 S002 W20 H130 S003 H101 S010 H111 S011 O00 O01 O02 O03 H121 S012 W21 H131 S013 H200 S100 H210 S101 O04 O05 O06 O07 H220 S110 H230 S111 H201 S102 H211 S103 H221 S112 H231 S113 S200 O10 O11 O12 O13 S201 S210 O14 O15 O16 O17 S211 S202 S203 S212 O20 O21 O22 O23 S213 O24 O25 O26 O27"
+DVE_DRAIN = "X0a X1a S201 S203 S211 S213 O25 O27"
+D_XQ, D_MUL, D_MQ, D_CAST, D_YQ = 1, 1, 1, 1, 2
+
+
+def tile_edge_messages_to_nodes_h3_kernel(tc, edge_feats, w_msg, edge_weight, incidence, bias, gain, out_0, out_1, out_2):
+    nc = tc.nc
+    dve_drain = set(DVE_DRAIN.split())
+    with ExitStack() as ctx:
+        keep = ctx.enter_context(tc.tile_pool(name="keep", bufs=1))
+        work = ctx.enter_context(tc.tile_pool(name="work", bufs=2))
+        psum = ctx.enter_context(tc.psum_pool(name="psum", bufs=1))
+        ctx.enter_context(tc.manual_schedule(engines={mybir.EngineType.PE}))
+
+        ident = keep.tile([P, P], F32, name="ident")
+        make_identity(nc, ident[:])
+
+        ew = keep.tile([P, EG, 4], BF16, name="ew")
+        nc.scalar.dma_start(out=ew[:], in_=edge_weight.rearrange("(g p t) -> p g t", p=P, t=4))
+        bias_raw = keep.tile([P, DG, 4], BF16, name="bias_raw")
+        nc.scalar.dma_start(out=bias_raw[:], in_=bias.rearrange("(g p t) -> p g t", p=P, t=4))
+        gain_raw = keep.tile([P, DG, 4], BF16, name="gain_raw")
+        nc.scalar.dma_start(out=gain_raw[:], in_=gain.rearrange("(g p t) -> p g t", p=P, t=4))
+        warm = keep.tile([P, 1], F32, name="warm")
+        nc.scalar.activation(out=warm[:], in_=ident[:, 0:1], func=ACT.Tanh)
+
+        x_raw, w_raw, inc_raw = {}, {}, {}
+
+        def load_x(g):
+            x_raw[g] = keep.tile([P, 4, DE], BF16, name="x_raw%d" % g)
+            nc.sync.dma_start(out=x_raw[g][:], in_=edge_feats[g * K : (g + 1) * K, :].rearrange("(m t) k -> m t k", t=4))
+
+        def load_w(g):
+            w_raw[g] = keep.tile([P, 4, K], BF16, name="w_raw%d" % g)
+            nc.sync.dma_start(out=w_raw[g][:], in_=w_msg[:, g * K : (g + 1) * K].rearrange("(p j) c -> p j c", j=4))
+
+        def load_inc(j):
+            inc_raw[j] = keep.tile([P, EDGES], BF16, name="inc_raw%d" % j)
+            nc.sync.dma_start(out=inc_raw[j][:], in_=incidence[j * P : (j + 1) * P, :])
+
+        load_x(0)
+        load_w(0)
+        for g in range(1, EG):
+            load_x(g)
+        for j in range(4):
+            load_inc(j)
+        load_w(1)
+        for j in range(4, NT):
+            load_inc(j)
+        load_w(2)
+
+        gain32 = keep.tile([P, DG * 4], F32, name="gain32")
+        nc.gpsimd.tensor_copy(out=gain32[:], in_=gain_raw[:].rearrange("p g t -> p (g t)"))
+        bg32 = keep.tile([P, DG * 4], F32, name="bg32")
+        nc.gpsimd.tensor_tensor(out=bg32[:], in0=bias_raw[:].rearrange("p g t -> p (g t)"), in1=gain_raw[:].rearrange("p g t -> p (g t)"), op=ALU.mult)
+
+        clock = [0]
+        pending = []
+
+        def later(delay, fn):
+            pending.append((clock[0] + delay, fn))
+
+        def tick():
+            clock[0] = clock[0] + 1
+            due = [e for e in pending if e[0] <= clock[0]]
+            for e in due:
+                pending.remove(e)
+                e[1]()
+
+        def new_bank():
+            b = clock[0] % 8
+            bank = psum.tile([P, 512], F32, name="bank%d" % b, tag="bank%d" % b)
+            return bank
+
+        def new_stage():
+            stage = work.tile([P, 2048], BF16, name="stage", tag="stage", bufs=4, align_bytes=64)
+            return stage
+
+        def codes_tiles(name, shape):
+            codes = keep.tile([P] + shape, U32, name=name + "_codes", align_bytes=64)
+            scales = keep.tile([P] + shape, U8, name=name + "_scales", align_bytes=64)
+            return codes, scales
+
+        def quantize(codes, scales, src):
+            nc.vector.quantize_mx(out=codes.bitcast(FP8X4), scales=scales, in_=src)
+
+        def move(key, out, in_):
+            if key in dve_drain:
+                nc.vector.tensor_copy(out=out, in_=in_)
+            else:
+                nc.scalar.copy(out=out, in_=in_)
+
+        xq, wq, msgq, incq, y_t = {}, {}, {}, {}, {}
+
+        def turn_pairs(key, words_of, then):
+            stage = new_stage()
+            dst = stage[:].bitcast(F32).rearrange("p (a m u) -> p a m u", a=4, u=2)
+            for b in range(2):
+                bank = new_bank()
+                view = bank[:].rearrange("p (a u m) -> p a u m", a=2, u=2)
+                for a in range(2):
+                    words = words_of(2 * b + a)
+                    for u in range(2):
+                        nc.tensor.transpose(view[:, a, u, :], words[:, u : 256 : 2], ident[:])
+                move(key + "ab"[b], dst[:, 2 * b : 2 * b + 2], view.rearrange("p a u m -> p a m u"))
+                if b == 1:
+                    later(D_XQ, lambda: then(stage))
+                tick()
+
+        def step_x(g):
+            xq[g] = codes_tiles("x%d" % g, [K])
+            turn_pairs("X%d" % g, lambda t: x_raw[g][:, t, :].bitcast(F32), lambda stage: quantize(xq[g][0][:], xq[g][1][:], stage[:]))
+
+        def step_inc(j):
+            h, jj = divmod(j, 4)
+            if jj == 0:
+                incq[h] = codes_tiles("inc%d" % h, [EG, K])
+
+            def then(stage):
+                for g in range(EG):
+                    quantize(incq[h][0][:, g, jj * P : (jj + 1) * P], incq[h][1][:, g, jj * P : (jj + 1) * P], stage[:, g * K : (g + 1) * K])
+
+            turn_pairs("I%d" % j, lambda g: inc_raw[j][:].bitcast(F32)[:, g * 256 : (g + 1) * 256], then)
+
+        def step_w(g, r):
+            if r == 0:
+                wq[g] = codes_tiles("w%d" % g, [K])
+            stage = work.tile([P, 1024], BF16, name="wstage", tag="wstage", bufs=2, align_bytes=64)
+            nc.vector.tensor_copy(out=stage[:].rearrange("p (t m j) -> p t m j", t=2, j=4), in_=w_raw[g][:].rearrange("p j (m t) -> p t m j", t=4)[:, 2 * r : 2 * r + 2])
+            later(1, lambda: quantize(wq[g][0][:, r * 256 : (r + 1) * 256], wq[g][1][:, r * 256 : (r + 1) * 256], stage[:]))
+
+        def step_msg(g, e, r):
+            codes, scales = codes_tiles("msg%d%d%d" % (g, e, r), [2 * P])
+            act = work.tile([P, 2, P, 4], F32, name="act", tag="act", bufs=4)
+            stage = work.tile([P, 1024], BF16, name="mstage", tag="mstage", bufs=4, align_bytes=64)
+
+            def weigh():
+                nc.vector.tensor_tensor(
+                    out=stage[:].rearrange("p (n s) -> p n s", s=4),
+                    in0=act[:].rearrange("p a n s -> p (a n) s"),
+                    in1=ew[:, e : e + 1, :].to_broadcast([P, 2 * P, 4]),
+                    op=ALU.mult,
+                )
+
+            for a in range(2):
+                t = 2 * r + a
+                msgq[(g, e, t)] = (codes[:, a * P : (a + 1) * P], scales[:, a * P : (a + 1) * P])
+                bank = new_bank()
+                for s in range(4):
+                    nc.tensor.matmul_mx(
+                        out=bank[:, s * P : (s + 1) * P],
+                        lhsT=xq[e][0][:, s * P : (s + 1) * P].bitcast(FP8X4),
+                        lhsT_scale=xq[e][1][:, s * P : (s + 1) * P],
+                        rhs=wq[g][0][:, t * P : (t + 1) * P].bitcast(FP8X4),
+                        rhs_scale=wq[g][1][:, t * P : (t + 1) * P],
+                        start=True,
+                        stop=True,
+                    )
+                nc.scalar.activation(out=act[:, a], in_=bank[:].rearrange("p (s n) -> p n s", s=4), func=ACT.Tanh)
+                if a == 1:
+                    later(D_MUL, weigh)
+                    later(D_MQ, lambda: quantize(codes[:], scales[:], stage[:]))
+                tick()
+
+        y_scales = {}
+
+        def planes(g, h):
+            stage = new_stage()
+            nc.vector.tensor_copy(
+                out=stage[:].rearrange("p (c i t) -> p c t i", i=4, t=4),
+                in_=y_t[(g, h)][:].rearrange("p t (c i) -> p c t i", i=4),
+            )
+
+            def finish():
+                if h == 0:
+                    y_scales[g] = keep.tile([P, NODES], U8, name="y_scales%d" % g, align_bytes=64)
+                y_codes = work.tile([P, K], U32, name="y_codes", tag="y_codes", bufs=3, align_bytes=64)
+                quantize(y_codes[:], y_scales[g][:, h * K : (h + 1) * K], stage[:])
+                nc.sync.dma_start(
+                    out=out_1[g, :, h * K : (h + 1) * K, :].rearrange("p m t -> p (m t)").bitcast(I32),
+                    in_=y_codes[:].bitcast(I32),
+                )
+                if h == 1:
+                    for quad in range(4):
+                        nc.sync.dma_start(
+                            out=out_2[g, 4 * quad : 4 * quad + 4, :].bitcast(I32),
+                            in_=y_scales[g][32 * quad : 32 * quad + 4, :].bitcast(I32),
+                        )
+
+            later(D_YQ - D_CAST, finish)
+
+        def step_sum(g, h, t):
+            if t == 0:
+                y_t[(g, h)] = work.tile([P, 4, K], F32, name="y_t", tag="y_t", bufs=3)
+            bank = new_bank()
+            for e in range(EG):
+                nc.tensor.matmul_mx(
+                    out=bank[:],
+                    lhsT=msgq[(g, e, t)][0].bitcast(FP8X4),
+                    lhsT_scale=msgq[(g, e, t)][1],
+                    rhs=incq[h][0][:, e, :].bitcast(FP8X4),
+                    rhs_scale=incq[h][1][:, e, :],
+                    start=(e == 0),
+                    stop=(e == EG - 1),
+                )
+            c = 4 * g + t
+            if "S%d%d%d" % (g, h, t) in dve_drain:
+                nc.vector.tensor_scalar(out=y_t[(g, h)][:, t, :], in0=bank[:], scalar1=gain32[:, c : c + 1], scalar2=bg32[:, c : c + 1], op0=ALU.mult, op1=ALU.add)
+            else:
+                nc.scalar.activation(out=y_t[(g, h)][:, t, :], in_=bank[:], func=ACT.Identity, bias=bg32[:, c : c + 1], scale=gain32[:, c : c + 1])
+            if t == 3:
+                later(D_CAST, lambda: planes(g, h))
+            tick()
+
+        def step_out(g, j):
+            h, jj = divmod(j, 4)
+            bank = new_bank()
+            for t in range(4):
+                nc.tensor.transpose(bank[:, t * P : (t + 1) * P], y_t[(g, h)][:, t, jj * P : (jj + 1) * P], ident[:])
+            y_sb = work.tile([P, K], F32, name="y_sb", tag="y_sb", bufs=6)
+            move("O%d%d" % (g, j), y_sb[:].rearrange("p (m t) -> p m t", t=4), bank[:].rearrange("p (t m) -> p m t", t=4))
+            nc.sync.dma_start(out=out_0[j * P : (j + 1) * P, g * K : (g + 1) * K], in_=y_sb[:])
+            tick()
+
+        for word in SEQ.split():
+            kind, n = word[0], word[1:]
+            if kind == "X":
+                step_x(int(n))
+            elif kind == "W":
+                step_w(int(n[0]), int(n[1]))
+            elif kind == "I":
+                step_inc(int(n))
+            elif kind == "H":
+                step_msg(int(n[0]), int(n[1]), int(n[2]))
+            elif kind == "S":
+                step_sum(int(n[0]), int(n[1]), int(n[2]))
+            else:
+                step_out(int(n[0]), int(n[1]))
+        for i in range(4):
+            tick()

@@ -21,9 +21,10 @@ EG = EDGES // K
 DG = DM // K
 NT = NODES // P
 
-SEQ = "W00 X0 X1 W01 H000 X2 H010 X3 H020 I0 H030 I1 H001 W10 I2 H011 I3 H021 W11 I4 H031 I5 H100 S000 I6 H110 S001 I7 H120 S002 W20 H130 S003 H101 S010 H111 S011 O00 O01 O02 O03 H121 S012 W21 H131 S013 H200 S100 H210 S101 O04 O05 O06 O07 H220 S110 H230 S111 H201 S102 H211 S103 H221 S112 H231 S113 S200 O10 O11 O12 O13 S201 S210 O14 O15 O16 O17 S211 S202 S203 S212 O20 O21 O22 O23 S213 O24 O25 O26 O27"
-DVE_DRAIN = "X0a X1a S201 S203 S211 S213 O25 O27"
+SEQ = "W00 X0 X1 H000 W01 X2 H010 X3 H020 I0 H030 W10 I1 H001 I2 H011 I3 H021 I4 H031 W11 I5 H100 S000 I6 H110 S001 I7 H120 S002 H130 W20 S003 H101 S010 H111 S011 H121 S012 H131 W21 S013 H200 S100 O00 O01 O02 O03 H210 S101 H220 S102 H230 S103 H201 S110 O04 O05 O06 O07 H211 S111 H221 S112 H231 S113 S200 O10 O11 O12 O13 S201 S210 S211 S202 O14 O15 O16 O17 S203 S212a O20 O21 O22 O23 S213a S212b S213b O24 O25 O26 O27"
+DVE_DRAIN = "O25 O27 S101 S103 S111 S113 S201 S203 S211 S213a S213b X0a X1a"
 D_XQ, D_MUL, D_MQ, D_CAST, D_YQ = 1, 1, 1, 1, 2
+WIDE = False
 
 
 def tile_edge_messages_to_nodes_h3_kernel(tc, edge_feats, w_msg, edge_weight, incidence, bias, gain, out_0, out_1, out_2):
@@ -38,44 +39,54 @@ def tile_edge_messages_to_nodes_h3_kernel(tc, edge_feats, w_msg, edge_weight, in
         ident = keep.tile([P, P], F32, name="ident")
         make_identity(nc, ident[:])
 
-        ew = keep.tile([P, EG, 4], BF16, name="ew")
-        nc.scalar.dma_start(out=ew[:], in_=edge_weight.rearrange("(g p t) -> p g t", p=P, t=4))
-        bias_raw = keep.tile([P, DG, 4], BF16, name="bias_raw")
-        nc.scalar.dma_start(out=bias_raw[:], in_=bias.rearrange("(g p t) -> p g t", p=P, t=4))
-        gain_raw = keep.tile([P, DG, 4], BF16, name="gain_raw")
-        nc.scalar.dma_start(out=gain_raw[:], in_=gain.rearrange("(g p t) -> p g t", p=P, t=4))
         warm = keep.tile([P, 1], F32, name="warm")
         nc.scalar.activation(out=warm[:], in_=ident[:, 0:1], func=ACT.Tanh)
 
         x_raw, w_raw, inc_raw = {}, {}, {}
 
-        def load_x(g):
-            x_raw[g] = keep.tile([P, 4, DE], BF16, name="x_raw%d" % g)
-            nc.sync.dma_start(out=x_raw[g][:], in_=edge_feats[g * K : (g + 1) * K, :].rearrange("(m t) k -> m t k", t=4))
+        def load_x(g, pieces):
+            rows = edge_feats[g * K : (g + 1) * K, :].rearrange("(m t) k -> m t k", t=4)
+            n = 4 // pieces
+            for i in range(pieces):
+                raw = keep.tile([P, n, DE], BF16, name="x_raw%d_%d" % (g, i))
+                nc.sync.dma_start(out=raw[:], in_=rows[:, i * n : (i + 1) * n, :])
+                for a in range(n):
+                    x_raw[(g, i * n + a)] = raw[:, a, :]
+
+        def load_vec(vec, name):
+            raw = keep.tile([P, vec.shape[0] // K, 4], BF16, name=name)
+            nc.sync.dma_start(out=raw[:], in_=vec.rearrange("(g p t) -> p g t", p=P, t=4))
+            return raw
 
         def load_w(g):
             w_raw[g] = keep.tile([P, 4, K], BF16, name="w_raw%d" % g)
             nc.sync.dma_start(out=w_raw[g][:], in_=w_msg[:, g * K : (g + 1) * K].rearrange("(p j) c -> p j c", j=4))
 
         def load_inc(j):
-            inc_raw[j] = keep.tile([P, EDGES], BF16, name="inc_raw%d" % j)
-            nc.sync.dma_start(out=inc_raw[j][:], in_=incidence[j * P : (j + 1) * P, :])
+            h, e = divmod(j, 4)
+            inc_raw[j] = keep.tile([P, 4, K], BF16, name="inc_raw%d" % j)
+            nc.sync.dma_start(out=inc_raw[j][:], in_=incidence[h * K : (h + 1) * K, e * K : (e + 1) * K].rearrange("(j n) k -> n j k", n=P))
 
-        load_x(0)
+        load_x(0, 2)
         load_w(0)
-        for g in range(1, EG):
-            load_x(g)
-        for j in range(4):
-            load_inc(j)
+        load_x(1, 1)
+        ew = load_vec(edge_weight, "ew")
+        for g in range(2, EG):
+            load_x(g, 1)
+        load_inc(0)
         load_w(1)
+        for j in range(1, 4):
+            load_inc(j)
+        bias_raw = load_vec(bias, "bias_raw")
+        gain_raw = load_vec(gain, "gain_raw")
         for j in range(4, NT):
             load_inc(j)
         load_w(2)
 
         gain32 = keep.tile([P, DG * 4], F32, name="gain32")
-        nc.gpsimd.tensor_copy(out=gain32[:], in_=gain_raw[:].rearrange("p g t -> p (g t)"))
+        nc.vector.tensor_copy(out=gain32[:], in_=gain_raw[:].rearrange("p g t -> p (g t)"))
         bg32 = keep.tile([P, DG * 4], F32, name="bg32")
-        nc.gpsimd.tensor_tensor(out=bg32[:], in0=bias_raw[:].rearrange("p g t -> p (g t)"), in1=gain_raw[:].rearrange("p g t -> p (g t)"), op=ALU.mult)
+        nc.vector.tensor_tensor(out=bg32[:], in0=bias_raw[:].rearrange("p g t -> p (g t)"), in1=gain_raw[:].rearrange("p g t -> p (g t)"), op=ALU.mult)
 
         clock = [0]
         pending = []
@@ -132,18 +143,11 @@ def tile_edge_messages_to_nodes_h3_kernel(tc, edge_feats, w_msg, edge_weight, in
 
         def step_x(g):
             xq[g] = codes_tiles("x%d" % g, [K])
-            turn_pairs("X%d" % g, lambda t: x_raw[g][:, t, :].bitcast(F32), lambda stage: quantize(xq[g][0][:], xq[g][1][:], stage[:]))
+            turn_pairs("X%d" % g, lambda t: x_raw[(g, t)].bitcast(F32), lambda stage: quantize(xq[g][0][:], xq[g][1][:], stage[:]))
 
         def step_inc(j):
-            h, jj = divmod(j, 4)
-            if jj == 0:
-                incq[h] = codes_tiles("inc%d" % h, [EG, K])
-
-            def then(stage):
-                for g in range(EG):
-                    quantize(incq[h][0][:, g, jj * P : (jj + 1) * P], incq[h][1][:, g, jj * P : (jj + 1) * P], stage[:, g * K : (g + 1) * K])
-
-            turn_pairs("I%d" % j, lambda g: inc_raw[j][:].bitcast(F32)[:, g * 256 : (g + 1) * 256], then)
+            incq[j] = codes_tiles("inc%d" % j, [K])
+            turn_pairs("I%d" % j, lambda a: inc_raw[j][:, a, :].bitcast(F32), lambda stage: quantize(incq[j][0][:], incq[j][1][:], stage[:]))
 
         def step_w(g, r):
             if r == 0:
@@ -154,32 +158,42 @@ def tile_edge_messages_to_nodes_h3_kernel(tc, edge_feats, w_msg, edge_weight, in
 
         def step_msg(g, e, r):
             codes, scales = codes_tiles("msg%d%d%d" % (g, e, r), [2 * P])
-            act = work.tile([P, 2, P, 4], F32, name="act", tag="act", bufs=4)
+            act = work.tile([P, 2, K], F32, name="act", tag="act", bufs=4)
             stage = work.tile([P, 1024], BF16, name="mstage", tag="mstage", bufs=4, align_bytes=64)
 
             def weigh():
-                nc.vector.tensor_tensor(
-                    out=stage[:].rearrange("p (n s) -> p n s", s=4),
-                    in0=act[:].rearrange("p a n s -> p (a n) s"),
-                    in1=ew[:, e : e + 1, :].to_broadcast([P, 2 * P, 4]),
-                    op=ALU.mult,
-                )
+                if WIDE:
+                    nc.vector.tensor_tensor(
+                        out=stage[:].rearrange("p (n a s) -> p n a s", a=2, s=2),
+                        in0=act[:].rearrange("p a (n s) -> p n a s", s=2),
+                        in1=ew[:, e : e + 1, :].rearrange("p o (a s) -> p o a s", s=2).to_broadcast([P, 2 * P, 2, 2]),
+                        op=ALU.mult,
+                    )
+                else:
+                    nc.vector.tensor_tensor(
+                        out=stage[:].rearrange("p (n s) -> p n s", s=4),
+                        in0=act[:].rearrange("p a (n s) -> p (a n) s", s=4),
+                        in1=ew[:, e : e + 1, :].to_broadcast([P, 2 * P, 4]),
+                        op=ALU.mult,
+                    )
 
             for a in range(2):
-                t = 2 * r + a
-                msgq[(g, e, t)] = (codes[:, a * P : (a + 1) * P], scales[:, a * P : (a + 1) * P])
+                msgq[(g, e, 2 * r + a)] = (codes[:, a * P : (a + 1) * P], scales[:, a * P : (a + 1) * P])
                 bank = new_bank()
-                for s in range(4):
+                slots = [2 * a, 2 * a + 1] if WIDE else [0, 1, 2, 3]
+                n = K // len(slots)
+                cols = slice(r * 256, (r + 1) * 256) if WIDE else slice((2 * r + a) * P, (2 * r + a + 1) * P)
+                for i, s in enumerate(slots):
                     nc.tensor.matmul_mx(
-                        out=bank[:, s * P : (s + 1) * P],
+                        out=bank[:, i * n : (i + 1) * n],
                         lhsT=xq[e][0][:, s * P : (s + 1) * P].bitcast(FP8X4),
                         lhsT_scale=xq[e][1][:, s * P : (s + 1) * P],
-                        rhs=wq[g][0][:, t * P : (t + 1) * P].bitcast(FP8X4),
-                        rhs_scale=wq[g][1][:, t * P : (t + 1) * P],
+                        rhs=wq[g][0][:, cols].bitcast(FP8X4),
+                        rhs_scale=wq[g][1][:, cols],
                         start=True,
                         stop=True,
                     )
-                nc.scalar.activation(out=act[:, a], in_=bank[:].rearrange("p (s n) -> p n s", s=4), func=ACT.Tanh)
+                nc.scalar.activation(out=act[:, a].rearrange("p (n s) -> p n s", s=len(slots)), in_=bank[:].rearrange("p (s n) -> p n s", s=len(slots)), func=ACT.Tanh)
                 if a == 1:
                     later(D_MUL, weigh)
                     later(D_MQ, lambda: quantize(codes[:], scales[:], stage[:]))
@@ -187,23 +201,24 @@ def tile_edge_messages_to_nodes_h3_kernel(tc, edge_feats, w_msg, edge_weight, in
 
         y_scales = {}
 
-        def planes(g, h):
+        def planes(g, h, n0, width):
             stage = new_stage()
             nc.vector.tensor_copy(
-                out=stage[:].rearrange("p (c i t) -> p c t i", i=4, t=4),
-                in_=y_t[(g, h)][:].rearrange("p t (c i) -> p c t i", i=4),
+                out=stage[:, : 4 * width].rearrange("p (c i t) -> p c t i", i=4, t=4),
+                in_=y_t[(g, h)][:, :, n0 : n0 + width].rearrange("p t (c i) -> p c t i", i=4),
             )
+            first = h * K + n0
 
             def finish():
-                if h == 0:
+                if first == 0:
                     y_scales[g] = keep.tile([P, NODES], U8, name="y_scales%d" % g, align_bytes=64)
                 y_codes = work.tile([P, K], U32, name="y_codes", tag="y_codes", bufs=3, align_bytes=64)
-                quantize(y_codes[:], y_scales[g][:, h * K : (h + 1) * K], stage[:])
+                quantize(y_codes[:, :width], y_scales[g][:, first : first + width], stage[:, : 4 * width])
                 nc.sync.dma_start(
-                    out=out_1[g, :, h * K : (h + 1) * K, :].rearrange("p m t -> p (m t)").bitcast(I32),
-                    in_=y_codes[:].bitcast(I32),
+                    out=out_1[g, :, first : first + width, :].rearrange("p m t -> p (m t)").bitcast(I32),
+                    in_=y_codes[:, :width].bitcast(I32),
                 )
-                if h == 1:
+                if first + width == NODES:
                     for quad in range(4):
                         nc.sync.dma_start(
                             out=out_2[g, 4 * quad : 4 * quad + 4, :].bitcast(I32),
@@ -212,27 +227,28 @@ def tile_edge_messages_to_nodes_h3_kernel(tc, edge_feats, w_msg, edge_weight, in
 
             later(D_YQ - D_CAST, finish)
 
-        def step_sum(g, h, t):
+        def step_sum(word, g, h, t, n0, width):
             if t == 0:
                 y_t[(g, h)] = work.tile([P, 4, K], F32, name="y_t", tag="y_t", bufs=3)
             bank = new_bank()
             for e in range(EG):
                 nc.tensor.matmul_mx(
-                    out=bank[:],
+                    out=bank[:, :width],
                     lhsT=msgq[(g, e, t)][0].bitcast(FP8X4),
                     lhsT_scale=msgq[(g, e, t)][1],
-                    rhs=incq[h][0][:, e, :].bitcast(FP8X4),
-                    rhs_scale=incq[h][1][:, e, :],
+                    rhs=incq[4 * h + e][0][:, n0 : n0 + width].bitcast(FP8X4),
+                    rhs_scale=incq[4 * h + e][1][:, n0 : n0 + width],
                     start=(e == 0),
                     stop=(e == EG - 1),
                 )
             c = 4 * g + t
-            if "S%d%d%d" % (g, h, t) in dve_drain:
-                nc.vector.tensor_scalar(out=y_t[(g, h)][:, t, :], in0=bank[:], scalar1=gain32[:, c : c + 1], scalar2=bg32[:, c : c + 1], op0=ALU.mult, op1=ALU.add)
+            dst = y_t[(g, h)][:, t, n0 : n0 + width]
+            if word in dve_drain:
+                nc.vector.tensor_scalar(out=dst, in0=bank[:, :width], scalar1=gain32[:, c : c + 1], scalar2=bg32[:, c : c + 1], op0=ALU.mult, op1=ALU.add)
             else:
-                nc.scalar.activation(out=y_t[(g, h)][:, t, :], in_=bank[:], func=ACT.Identity, bias=bg32[:, c : c + 1], scale=gain32[:, c : c + 1])
+                nc.scalar.activation(out=dst, in_=bank[:, :width], func=ACT.Identity, bias=bg32[:, c : c + 1], scale=gain32[:, c : c + 1])
             if t == 3:
-                later(D_CAST, lambda: planes(g, h))
+                later(D_CAST, lambda: planes(g, h, n0, width))
             tick()
 
         def step_out(g, j):
@@ -256,7 +272,7 @@ def tile_edge_messages_to_nodes_h3_kernel(tc, edge_feats, w_msg, edge_weight, in
             elif kind == "H":
                 step_msg(int(n[0]), int(n[1]), int(n[2]))
             elif kind == "S":
-                step_sum(int(n[0]), int(n[1]), int(n[2]))
+                step_sum(word, int(n[0]), int(n[1]), int(n[2]), 256 if n[3:] == "b" else 0, 256 if n[3:] else 512)
             else:
                 step_out(int(n[0]), int(n[1]))
         for i in range(4):

@@ -16,264 +16,284 @@ ACT = mybir.ActivationFunctionType
 ALU = mybir.AluOpType
 
 P = 128
-K = 512
-EG = EDGES // K
-DG = DM // K
-NT = NODES // P
+SLOTS = 4
+PASS = P * SLOTS
+BANK = 512
+BANKS = 8
+EDGE_GROUPS = EDGES // PASS
+FEATURE_GROUPS = DM // PASS
+HALF = NODES // 2
+QUARTER = HALF // 2
 
-SEQ = "W00 X0 X1 H000 W01 X2 H010 X3 H020 I0 H030 W10 I1 H001 I2 H011 I3 H021 I4 H031 W11 I5 H100 S000 I6 H110 S001 I7 H120 S002 H130 W20 S003 H101 S010 H111 S011 H121 S012 H131 W21 S013 H200 S100 O00 O01 O02 O03 H210 S101 H220 S102 H230 S103 H201 S110 O04 O05 O06 O07 H211 S111 H221 S112 H231 S113 S200 O10 O11 O12 O13 S201 S210 S211 S202 O14 O15 O16 O17 S203 S212a O20 O21 O22 O23 S213a S212b S213b O24 O25 O26 O27"
-DVE_DRAIN = "O25 O27 S101 S103 S111 S113 S201 S203 S211 S213a S213b X0a X1a"
-D_XQ, D_MUL, D_MQ, D_CAST, D_YQ = 1, 1, 1, 1, 2
-WIDE = False
+SUM_START = 11
+OUT_DELAY = 5
+VECTOR_SUMS_FROM = 8
+VECTOR_TURN_EVERY = 4
+READ_LAG = 3
+QUANT_LAG = 4
+WLAG = 1
 
 
-def tile_edge_messages_to_nodes_h3_kernel(tc, edge_feats, w_msg, edge_weight, incidence, bias, gain, out_0, out_1, out_2):
+def tile_edge_messages_to_nodes_h3_kernel(
+    tc, edge_feats, w_msg, edge_weight, incidence, bias, gain, out_0, out_1, out_2
+):
     nc = tc.nc
-    dve_drain = set(DVE_DRAIN.split())
     with ExitStack() as ctx:
         keep = ctx.enter_context(tc.tile_pool(name="keep", bufs=1))
         work = ctx.enter_context(tc.tile_pool(name="work", bufs=2))
         psum = ctx.enter_context(tc.psum_pool(name="psum", bufs=1))
-        ctx.enter_context(tc.manual_schedule(engines={mybir.EngineType.PE}))
+        ctx.enter_context(tc.manual_schedule())
 
         ident = keep.tile([P, P], F32, name="ident")
         make_identity(nc, ident[:])
 
-        warm = keep.tile([P, 1], F32, name="warm")
-        nc.scalar.activation(out=warm[:], in_=ident[:, 0:1], func=ACT.Tanh)
+        turn_rows, w_raw = {}, {}
 
-        x_raw, w_raw, inc_raw = {}, {}, {}
-
-        def load_x(g, pieces):
-            rows = edge_feats[g * K : (g + 1) * K, :].rearrange("(m t) k -> m t k", t=4)
-            n = 4 // pieces
+        def load_feats(e, pieces):
+            rows = edge_feats[e * PASS : (e + 1) * PASS, :].rearrange("(m s) k -> m s k", s=SLOTS)
+            n = SLOTS // pieces
+            turn_rows[e] = []
             for i in range(pieces):
-                raw = keep.tile([P, n, DE], BF16, name="x_raw%d_%d" % (g, i))
+                raw = keep.tile([P, n, DE], BF16, name="feats%d_%d" % (e, i))
                 nc.sync.dma_start(out=raw[:], in_=rows[:, i * n : (i + 1) * n, :])
-                for a in range(n):
-                    x_raw[(g, i * n + a)] = raw[:, a, :]
+                turn_rows[e].extend([raw[:, a, :] for a in range(n)])
 
-        def load_vec(vec, name):
-            raw = keep.tile([P, vec.shape[0] // K, 4], BF16, name=name)
-            nc.sync.dma_start(out=raw[:], in_=vec.rearrange("(g p t) -> p g t", p=P, t=4))
-            return raw
+        def load_incidence(h, e):
+            raw = keep.tile([P, 4, PASS], BF16, name="inc%d_%d" % (h, e))
+            rows = incidence[h * HALF : (h + 1) * HALF, e * PASS : (e + 1) * PASS]
+            nc.sync.dma_start(out=raw[:], in_=rows.rearrange("(a n) k -> n a k", n=P))
+            turn_rows[EDGE_GROUPS * (h + 1) + e] = [raw[:, a, :] for a in range(4)]
 
         def load_w(g):
-            w_raw[g] = keep.tile([P, 4, K], BF16, name="w_raw%d" % g)
-            nc.sync.dma_start(out=w_raw[g][:], in_=w_msg[:, g * K : (g + 1) * K].rearrange("(p j) c -> p j c", j=4))
+            w_raw[g] = keep.tile([P, SLOTS, PASS], BF16, name="w_raw%d" % g)
+            cols = w_msg[:, g * PASS : (g + 1) * PASS]
+            nc.sync.dma_start(out=w_raw[g][:], in_=cols.rearrange("(p j) c -> p j c", j=SLOTS))
 
-        def load_inc(j):
-            h, e = divmod(j, 4)
-            inc_raw[j] = keep.tile([P, 4, K], BF16, name="inc_raw%d" % j)
-            nc.sync.dma_start(out=inc_raw[j][:], in_=incidence[h * K : (h + 1) * K, e * K : (e + 1) * K].rearrange("(j n) k -> n j k", n=P))
+        def load_by_slot(vec, name):
+            raw = keep.tile([P, vec.shape[0] // PASS, SLOTS], BF16, name=name)
+            nc.sync.dma_start(out=raw[:], in_=vec.rearrange("(g p t) -> p g t", p=P, t=SLOTS))
+            return raw
 
-        load_x(0, 2)
+        load_feats(0, 2)
         load_w(0)
-        load_x(1, 1)
-        ew = load_vec(edge_weight, "ew")
-        for g in range(2, EG):
-            load_x(g, 1)
-        load_inc(0)
+        load_feats(1, 1)
+        weight = load_by_slot(edge_weight, "weight")
         load_w(1)
-        for j in range(1, 4):
-            load_inc(j)
-        bias_raw = load_vec(bias, "bias_raw")
-        gain_raw = load_vec(gain, "gain_raw")
-        for j in range(4, NT):
-            load_inc(j)
+        load_feats(2, 1)
         load_w(2)
+        load_feats(3, 1)
+        for e in range(EDGE_GROUPS):
+            load_incidence(0, e)
+        bias_raw = load_by_slot(bias, "bias_raw")
+        gain_raw = load_by_slot(gain, "gain_raw")
+        for e in range(EDGE_GROUPS):
+            load_incidence(1, e)
 
-        gain32 = keep.tile([P, DG * 4], F32, name="gain32")
-        nc.vector.tensor_copy(out=gain32[:], in_=gain_raw[:].rearrange("p g t -> p (g t)"))
-        bg32 = keep.tile([P, DG * 4], F32, name="bg32")
-        nc.vector.tensor_tensor(out=bg32[:], in0=bias_raw[:].rearrange("p g t -> p (g t)"), in1=gain_raw[:].rearrange("p g t -> p (g t)"), op=ALU.mult)
+        gain32 = keep.tile([P, FEATURE_GROUPS * SLOTS], F32, name="gain32")
+        bias_gain = keep.tile([P, FEATURE_GROUPS * SLOTS], F32, name="bias_gain")
 
-        clock = [0]
+        def prepare_factors():
+            nc.vector.tensor_copy(out=gain32[:], in_=gain_raw[:].rearrange("p g t -> p (g t)"))
+            nc.vector.tensor_tensor(
+                out=bias_gain[:],
+                in0=bias_raw[:].rearrange("p g t -> p (g t)"),
+                in1=gain_raw[:].rearrange("p g t -> p (g t)"),
+                op=ALU.mult,
+            )
+
+        banks_taken = []
         pending = []
 
-        def later(delay, fn):
-            pending.append((clock[0] + delay, fn))
+        def later(lag, emit):
+            pending.append((len(banks_taken) - 1 + lag, emit))
 
-        def tick():
-            clock[0] = clock[0] + 1
-            due = [e for e in pending if e[0] <= clock[0]]
-            for e in due:
-                pending.remove(e)
-                e[1]()
+        def emit_due(bank_number):
+            for entry in sorted([e for e in pending if e[0] <= bank_number], key=lambda e: e[0]):
+                pending.remove(entry)
+                entry[1]()
 
-        def new_bank():
-            b = clock[0] % 8
-            bank = psum.tile([P, 512], F32, name="bank%d" % b, tag="bank%d" % b)
+        def next_bank():
+            emit_due(len(banks_taken))
+            tag = "bank%d" % (len(banks_taken) % BANKS)
+            banks_taken.append(tag)
+            bank = psum.tile([P, BANK], F32, name=tag, tag=tag)
             return bank
 
-        def new_stage():
-            stage = work.tile([P, 2048], BF16, name="stage", tag="stage", bufs=4, align_bytes=64)
+        def wide_stage():
+            stage = work.tile([P, PASS * SLOTS], BF16, name="stage", tag="stage", bufs=4, align_bytes=64)
             return stage
 
-        def codes_tiles(name, shape):
-            codes = keep.tile([P] + shape, U32, name=name + "_codes", align_bytes=64)
-            scales = keep.tile([P] + shape, U8, name=name + "_scales", align_bytes=64)
+        def operand(name, columns):
+            codes = keep.tile([P, columns], U32, name=name + "_codes", align_bytes=64)
+            scales = keep.tile([P, columns], U8, name=name + "_scales", align_bytes=64)
             return codes, scales
 
-        def quantize(codes, scales, src):
-            nc.vector.quantize_mx(out=codes.bitcast(FP8X4), scales=scales, in_=src)
+        def quantize(codes, scales, values):
+            nc.vector.quantize_mx(out=codes.bitcast(FP8X4), scales=scales, in_=values)
 
-        def move(key, out, in_):
-            if key in dve_drain:
+        def product(out, stationary, moving, start, stop):
+            nc.tensor.matmul_mx(
+                out=out,
+                lhsT=stationary[0].bitcast(FP8X4),
+                lhsT_scale=stationary[1],
+                rhs=moving[0].bitcast(FP8X4),
+                rhs_scale=moving[1],
+                start=start,
+                stop=stop,
+            )
+
+        def columns(pair, first, count):
+            return pair[0][:, first : first + count], pair[1][:, first : first + count]
+
+        def copy_out(on_vector, out, in_):
+            if on_vector:
                 nc.vector.tensor_copy(out=out, in_=in_)
             else:
                 nc.scalar.copy(out=out, in_=in_)
 
-        xq, wq, msgq, incq, y_t = {}, {}, {}, {}, {}
+        turned, w_q, msg_q, y_t, y_scales = {}, {}, {}, {}, {}
 
-        def turn_pairs(key, words_of, then):
-            stage = new_stage()
-            dst = stage[:].bitcast(F32).rearrange("p (a m u) -> p a m u", a=4, u=2)
+        def turn(i):
+            turned[i] = operand("turned%d" % i, PASS)
+            stage = wide_stage()
+            words_out = stage[:].bitcast(F32).rearrange("p (a n u) -> p a n u", a=4, u=2)
             for b in range(2):
-                bank = new_bank()
-                view = bank[:].rearrange("p (a u m) -> p a u m", a=2, u=2)
+                bank = next_bank()
+                view = bank[:].rearrange("p (a u n) -> p a u n", a=2, u=2)
                 for a in range(2):
-                    words = words_of(2 * b + a)
+                    words = turn_rows[i][2 * b + a].bitcast(F32)
                     for u in range(2):
-                        nc.tensor.transpose(view[:, a, u, :], words[:, u : 256 : 2], ident[:])
-                move(key + "ab"[b], dst[:, 2 * b : 2 * b + 2], view.rearrange("p a u m -> p a m u"))
-                if b == 1:
-                    later(D_XQ, lambda: then(stage))
-                tick()
+                        nc.tensor.transpose(view[:, a, u, :], words[:, u : PASS // 2 : 2], ident[:])
+                on_vector = b == 1 and i % VECTOR_TURN_EVERY == VECTOR_TURN_EVERY - 1
+                copy_out(on_vector, words_out[:, 2 * b : 2 * b + 2], view.rearrange("p a u n -> p a n u"))
+            later(1 if i < EDGE_GROUPS else QUANT_LAG, lambda: quantize(turned[i][0][:], turned[i][1][:], stage[:]))
 
-        def step_x(g):
-            xq[g] = codes_tiles("x%d" % g, [K])
-            turn_pairs("X%d" % g, lambda t: x_raw[(g, t)].bitcast(F32), lambda stage: quantize(xq[g][0][:], xq[g][1][:], stage[:]))
+        def prepare_w(g):
+            w_q[g] = operand("w%d" % g, PASS)
+            stages = []
+            for r in range(2):
+                stage = work.tile([P, 2 * P * SLOTS], BF16, name="w_stage", tag="w_stage", bufs=3, align_bytes=64)
+                nc.vector.tensor_copy(
+                    out=stage[:].rearrange("p (t c m j) -> p c j t m", t=2, m=2, j=SLOTS),
+                    in_=w_raw[g][:].rearrange("p j (c m t) -> p c j t m", m=2, t=SLOTS)[:, :, :, 2 * r : 2 * r + 2, :],
+                )
+                stages.append(stage)
+            for r in range(2):
+                later(WLAG, lambda r=r: quantize(*columns(w_q[g], r * 2 * P, 2 * P), stages[r][:]))
 
-        def step_inc(j):
-            incq[j] = codes_tiles("inc%d" % j, [K])
-            turn_pairs("I%d" % j, lambda a: inc_raw[j][:, a, :].bitcast(F32), lambda stage: quantize(incq[j][0][:], incq[j][1][:], stage[:]))
-
-        def step_w(g, r):
-            if r == 0:
-                wq[g] = codes_tiles("w%d" % g, [K])
-            stage = work.tile([P, 1024], BF16, name="wstage", tag="wstage", bufs=2, align_bytes=64)
-            nc.vector.tensor_copy(out=stage[:].rearrange("p (t m j) -> p t m j", t=2, j=4), in_=w_raw[g][:].rearrange("p j (m t) -> p t m j", t=4)[:, 2 * r : 2 * r + 2])
-            later(1, lambda: quantize(wq[g][0][:, r * 256 : (r + 1) * 256], wq[g][1][:, r * 256 : (r + 1) * 256], stage[:]))
-
-        def step_msg(g, e, r):
-            codes, scales = codes_tiles("msg%d%d%d" % (g, e, r), [2 * P])
-            act = work.tile([P, 2, K], F32, name="act", tag="act", bufs=4)
-            stage = work.tile([P, 1024], BF16, name="mstage", tag="mstage", bufs=4, align_bytes=64)
-
-            def weigh():
-                if WIDE:
-                    nc.vector.tensor_tensor(
-                        out=stage[:].rearrange("p (n a s) -> p n a s", a=2, s=2),
-                        in0=act[:].rearrange("p a (n s) -> p n a s", s=2),
-                        in1=ew[:, e : e + 1, :].rearrange("p o (a s) -> p o a s", s=2).to_broadcast([P, 2 * P, 2, 2]),
-                        op=ALU.mult,
-                    )
-                else:
-                    nc.vector.tensor_tensor(
-                        out=stage[:].rearrange("p (n s) -> p n s", s=4),
-                        in0=act[:].rearrange("p a (n s) -> p (a n) s", s=4),
-                        in1=ew[:, e : e + 1, :].to_broadcast([P, 2 * P, 4]),
-                        op=ALU.mult,
-                    )
-
+        def message(g, e, r):
+            quantised = operand("msg%d%d%d" % (g, e, r), 2 * P)
             for a in range(2):
-                msgq[(g, e, 2 * r + a)] = (codes[:, a * P : (a + 1) * P], scales[:, a * P : (a + 1) * P])
-                bank = new_bank()
-                slots = [2 * a, 2 * a + 1] if WIDE else [0, 1, 2, 3]
-                n = K // len(slots)
-                cols = slice(r * 256, (r + 1) * 256) if WIDE else slice((2 * r + a) * P, (2 * r + a + 1) * P)
-                for i, s in enumerate(slots):
-                    nc.tensor.matmul_mx(
-                        out=bank[:, i * n : (i + 1) * n],
-                        lhsT=xq[e][0][:, s * P : (s + 1) * P].bitcast(FP8X4),
-                        lhsT_scale=xq[e][1][:, s * P : (s + 1) * P],
-                        rhs=wq[g][0][:, cols].bitcast(FP8X4),
-                        rhs_scale=wq[g][1][:, cols],
-                        start=True,
-                        stop=True,
+                msg_q[(g, e, 2 * r + a)] = columns(quantised, a * P, P)
+            act = work.tile([P, 2, 2 * P, 2], F32, name="act", tag="act", bufs=4)
+            for b in range(2):
+                bank = next_bank()
+                for i in range(2):
+                    product(
+                        bank[:, i * 2 * P : (i + 1) * 2 * P],
+                        columns(turned[e], (2 * b + i) * P, P),
+                        columns(w_q[g], r * 2 * P, 2 * P),
+                        True,
+                        True,
                     )
-                nc.scalar.activation(out=act[:, a].rearrange("p (n s) -> p n s", s=len(slots)), in_=bank[:].rearrange("p (s n) -> p n s", s=len(slots)), func=ACT.Tanh)
-                if a == 1:
-                    later(D_MUL, weigh)
-                    later(D_MQ, lambda: quantize(codes[:], scales[:], stage[:]))
-                tick()
+                nc.scalar.activation(out=act[:, b], in_=bank[:].rearrange("p (i n) -> p n i", i=2), func=ACT.Tanh)
+            stage = work.tile([P, 2 * P * SLOTS], BF16, name="msg_stage", tag="msg_stage", bufs=4, align_bytes=64)
+            by_slot = weight[:, e : e + 1, :].rearrange("p o (b i) -> p o b i", i=2)
+            later(
+                READ_LAG,
+                lambda: nc.vector.tensor_tensor(
+                    out=stage[:].rearrange("p (n b i) -> p n b i", b=2, i=2),
+                    in0=act[:].rearrange("p b n i -> p n b i"),
+                    in1=by_slot.to_broadcast([P, 2 * P, 2, 2]),
+                    op=ALU.mult,
+                ),
+            )
+            later(READ_LAG + QUANT_LAG, lambda: quantize(quantised[0][:], quantised[1][:], stage[:]))
 
-        y_scales = {}
-
-        def planes(g, h, n0, width):
-            stage = new_stage()
+        def round_planes(g, h, n0, width):
+            stage = wide_stage()
             nc.vector.tensor_copy(
-                out=stage[:, : 4 * width].rearrange("p (c i t) -> p c t i", i=4, t=4),
+                out=stage[:, : SLOTS * width].rearrange("p (c i t) -> p c t i", i=4, t=SLOTS),
                 in_=y_t[(g, h)][:, :, n0 : n0 + width].rearrange("p t (c i) -> p c t i", i=4),
             )
-            first = h * K + n0
+            return stage
 
-            def finish():
-                if first == 0:
-                    y_scales[g] = keep.tile([P, NODES], U8, name="y_scales%d" % g, align_bytes=64)
-                y_codes = work.tile([P, K], U32, name="y_codes", tag="y_codes", bufs=3, align_bytes=64)
-                quantize(y_codes[:, :width], y_scales[g][:, first : first + width], stage[:, : 4 * width])
-                nc.sync.dma_start(
-                    out=out_1[g, :, first : first + width, :].rearrange("p m t -> p (m t)").bitcast(I32),
-                    in_=y_codes[:, :width].bitcast(I32),
-                )
-                if first + width == NODES:
-                    for quad in range(4):
-                        nc.sync.dma_start(
-                            out=out_2[g, 4 * quad : 4 * quad + 4, :].bitcast(I32),
-                            in_=y_scales[g][32 * quad : 32 * quad + 4, :].bitcast(I32),
-                        )
+        def store_planes(g, first, width, stage):
+            if first == 0:
+                y_scales[g] = keep.tile([P, NODES], U8, name="y_scales%d" % g, align_bytes=64)
+            y_codes = work.tile([P, HALF], U32, name="y_codes", tag="y_codes", bufs=3, align_bytes=64)
+            quantize(y_codes[:, :width], y_scales[g][:, first : first + width], stage[:, : SLOTS * width])
+            nc.sync.dma_start(
+                out=out_1[g, :, first : first + width, :].rearrange("p m t -> p (m t)").bitcast(I32),
+                in_=y_codes[:, :width].bitcast(I32),
+            )
+            if first + width == NODES:
+                for quad in range(4):
+                    nc.sync.dma_start(
+                        out=out_2[g, 4 * quad : 4 * quad + 4, :].bitcast(I32),
+                        in_=y_scales[g][32 * quad : 32 * quad + 4, :].bitcast(I32),
+                    )
 
-            later(D_YQ - D_CAST, finish)
-
-        def step_sum(word, g, h, t, n0, width):
+        def node_sum(on_vector, g, h, t, n0, width):
             if t == 0:
-                y_t[(g, h)] = work.tile([P, 4, K], F32, name="y_t", tag="y_t", bufs=3)
-            bank = new_bank()
-            for e in range(EG):
-                nc.tensor.matmul_mx(
-                    out=bank[:, :width],
-                    lhsT=msgq[(g, e, t)][0].bitcast(FP8X4),
-                    lhsT_scale=msgq[(g, e, t)][1],
-                    rhs=incq[4 * h + e][0][:, n0 : n0 + width].bitcast(FP8X4),
-                    rhs_scale=incq[4 * h + e][1][:, n0 : n0 + width],
-                    start=(e == 0),
-                    stop=(e == EG - 1),
+                y_t[(g, h)] = work.tile([P, SLOTS, HALF], F32, name="y_t", tag="y_t", bufs=3)
+            bank = next_bank()
+            for e in range(EDGE_GROUPS):
+                nodes = columns(turned[EDGE_GROUPS * (h + 1) + e], n0, width)
+                product(bank[:, :width], msg_q[(g, e, t)], nodes, e == 0, e == EDGE_GROUPS - 1)
+            c = SLOTS * g + t
+            factor, term = gain32[:, c : c + 1], bias_gain[:, c : c + 1]
+            out = y_t[(g, h)][:, t, n0 : n0 + width]
+            if on_vector:
+                nc.vector.tensor_scalar(
+                    out=out, in0=bank[:, :width], scalar1=factor, scalar2=term, op0=ALU.mult, op1=ALU.add
                 )
-            c = 4 * g + t
-            dst = y_t[(g, h)][:, t, n0 : n0 + width]
-            if word in dve_drain:
-                nc.vector.tensor_scalar(out=dst, in0=bank[:, :width], scalar1=gain32[:, c : c + 1], scalar2=bg32[:, c : c + 1], op0=ALU.mult, op1=ALU.add)
             else:
-                nc.scalar.activation(out=dst, in_=bank[:, :width], func=ACT.Identity, bias=bg32[:, c : c + 1], scale=gain32[:, c : c + 1])
-            if t == 3:
-                later(D_CAST, lambda: planes(g, h, n0, width))
-            tick()
+                nc.scalar.activation(out=out, in_=bank[:, :width], func=ACT.Identity, bias=term, scale=factor)
+            if t == SLOTS - 1:
+                rounded = []
+                later(READ_LAG, lambda: rounded.append(round_planes(g, h, n0, width)))
+                later(READ_LAG + QUANT_LAG, lambda: store_planes(g, h * HALF + n0, width, rounded[0]))
 
-        def step_out(g, j):
-            h, jj = divmod(j, 4)
-            bank = new_bank()
-            for t in range(4):
-                nc.tensor.transpose(bank[:, t * P : (t + 1) * P], y_t[(g, h)][:, t, jj * P : (jj + 1) * P], ident[:])
-            y_sb = work.tile([P, K], F32, name="y_sb", tag="y_sb", bufs=6)
-            move("O%d%d" % (g, j), y_sb[:].rearrange("p (m t) -> p m t", t=4), bank[:].rearrange("p (t m) -> p m t", t=4))
-            nc.sync.dma_start(out=out_0[j * P : (j + 1) * P, g * K : (g + 1) * K], in_=y_sb[:])
-            tick()
+        def store_rows(g, h, share_with_vector):
+            for a in range(4):
+                bank = next_bank()
+                for t in range(SLOTS):
+                    nc.tensor.transpose(bank[:, t * P : (t + 1) * P], y_t[(g, h)][:, t, a * P : (a + 1) * P], ident[:])
+                rows = work.tile([P, PASS], F32, name="rows", tag="rows", bufs=6)
+                copy_out(
+                    share_with_vector and a % 2 == 1,
+                    rows[:].rearrange("p (m t) -> p m t", t=SLOTS),
+                    bank[:].rearrange("p (t m) -> p m t", t=SLOTS),
+                )
+                node0 = h * HALF + a * P
+                nc.sync.dma_start(out=out_0[node0 : node0 + P, g * PASS : (g + 1) * PASS], in_=rows[:])
 
-        for word in SEQ.split():
-            kind, n = word[0], word[1:]
-            if kind == "X":
-                step_x(int(n))
-            elif kind == "W":
-                step_w(int(n[0]), int(n[1]))
-            elif kind == "I":
-                step_inc(int(n))
-            elif kind == "H":
-                step_msg(int(n[0]), int(n[1]), int(n[2]))
-            elif kind == "S":
-                step_sum(word, int(n[0]), int(n[1]), int(n[2]), 256 if n[3:] == "b" else 0, 256 if n[3:] else 512)
-            else:
-                step_out(int(n[0]), int(n[1]))
-        for i in range(4):
-            tick()
+        last = FEATURE_GROUPS - 1
+        messages = [(0, e, r) for e in range(EDGE_GROUPS) for r in range(2)]
+        messages += [(g, e, r) for g in range(1, FEATURE_GROUPS) for r in range(2) for e in range(EDGE_GROUPS)]
+        sums = [(g, h, t, 0, HALF) for g in range(last) for h in range(2) for t in range(SLOTS)]
+        sums += [(last, h, t, 0, HALF) for h in range(2) for t in (0, 1)]
+        sums += [(last, 0, t, 0, HALF) for t in (2, 3)]
+        sums += [(last, 1, t, n0, QUARTER) for n0 in (0, QUARTER) for t in (2, 3)]
+        out_after = {}
+        for j, (g, h, t, n0, width) in enumerate(sums):
+            if t == SLOTS - 1 and n0 + width == HALF:
+                out_after[j + (OUT_DELAY if g < last else 2 - 2 * h)] = (g, h)
+
+        prepare_w(0)
+        for i in range(SUM_START + len(sums)):
+            j = i - SUM_START
+            if j == -1:
+                prepare_factors()
+            if j >= 0:
+                node_sum(j >= VECTOR_SUMS_FROM and j % 2 == 1, *sums[j])
+                if j in out_after:
+                    store_rows(*out_after[j], out_after[j] == (last, 1))
+            if i in turn_rows:
+                turn(i)
+            if 1 <= i < FEATURE_GROUPS:
+                prepare_w(i)
+            if 1 <= i <= len(messages):
+                message(*messages[i - 1])
+        emit_due(len(banks_taken) + READ_LAG + QUANT_LAG)

from contextlib import ExitStack

import concourse.mybir as mybir
from concourse.masks import make_identity

EDGES, NODES, DE, DM = 2048, 1024, 512, 1536
FLOPS = 2 * EDGES * DE * DM + 2 * NODES * EDGES * DM

F32 = mybir.dt.float32
BF16 = mybir.dt.bfloat16
U32 = mybir.dt.uint32
I32 = mybir.dt.int32
U8 = mybir.dt.uint8
FP8X4 = mybir.dt.float8_e4m3fn_x4
ACT = mybir.ActivationFunctionType
ALU = mybir.AluOpType

P = 128
SLOTS = 4
PASS = P * SLOTS
BANK = 512
BANKS = 8
EDGE_GROUPS = EDGES // PASS
FEATURE_GROUPS = DM // PASS
HALF = NODES // 2
QUARTER = HALF // 2

SUM_START = 11
OUT_DELAY = 5
VECTOR_SUMS_FROM = 8
VECTOR_TURN_EVERY = 4
READ_LAG = 3
QUANT_LAG = 4
WLAG = 1


def tile_edge_messages_to_nodes_h3_kernel(
    tc, edge_feats, w_msg, edge_weight, incidence, bias, gain, out_0, out_1, out_2
):
    nc = tc.nc
    with ExitStack() as ctx:
        keep = ctx.enter_context(tc.tile_pool(name="keep", bufs=1))
        work = ctx.enter_context(tc.tile_pool(name="work", bufs=2))
        psum = ctx.enter_context(tc.psum_pool(name="psum", bufs=1))
        ctx.enter_context(tc.manual_schedule())

        ident = keep.tile([P, P], F32, name="ident")
        make_identity(nc, ident[:])

        turn_rows, w_raw = {}, {}

        def load_feats(e, pieces):
            rows = edge_feats[e * PASS : (e + 1) * PASS, :].rearrange("(m s) k -> m s k", s=SLOTS)
            n = SLOTS // pieces
            turn_rows[e] = []
            for i in range(pieces):
                raw = keep.tile([P, n, DE], BF16, name="feats%d_%d" % (e, i))
                nc.sync.dma_start(out=raw[:], in_=rows[:, i * n : (i + 1) * n, :])
                turn_rows[e].extend([raw[:, a, :] for a in range(n)])

        def load_incidence(h, e):
            raw = keep.tile([P, 4, PASS], BF16, name="inc%d_%d" % (h, e))
            rows = incidence[h * HALF : (h + 1) * HALF, e * PASS : (e + 1) * PASS]
            nc.sync.dma_start(out=raw[:], in_=rows.rearrange("(a n) k -> n a k", n=P))
            turn_rows[EDGE_GROUPS * (h + 1) + e] = [raw[:, a, :] for a in range(4)]

        def load_w(g):
            w_raw[g] = keep.tile([P, SLOTS, PASS], BF16, name="w_raw%d" % g)
            cols = w_msg[:, g * PASS : (g + 1) * PASS]
            nc.sync.dma_start(out=w_raw[g][:], in_=cols.rearrange("(p j) c -> p j c", j=SLOTS))

        def load_by_slot(vec, name):
            raw = keep.tile([P, vec.shape[0] // PASS, SLOTS], BF16, name=name)
            nc.sync.dma_start(out=raw[:], in_=vec.rearrange("(g p t) -> p g t", p=P, t=SLOTS))
            return raw

        load_feats(0, 2)
        load_w(0)
        load_feats(1, 1)
        weight = load_by_slot(edge_weight, "weight")
        load_w(1)
        load_feats(2, 1)
        load_w(2)
        load_feats(3, 1)
        for e in range(EDGE_GROUPS):
            load_incidence(0, e)
        bias_raw = load_by_slot(bias, "bias_raw")
        gain_raw = load_by_slot(gain, "gain_raw")
        for e in range(EDGE_GROUPS):
            load_incidence(1, e)

        gain32 = keep.tile([P, FEATURE_GROUPS * SLOTS], F32, name="gain32")
        bias_gain = keep.tile([P, FEATURE_GROUPS * SLOTS], F32, name="bias_gain")

        def prepare_factors():
            nc.vector.tensor_copy(out=gain32[:], in_=gain_raw[:].rearrange("p g t -> p (g t)"))
            nc.vector.tensor_tensor(
                out=bias_gain[:],
                in0=bias_raw[:].rearrange("p g t -> p (g t)"),
                in1=gain_raw[:].rearrange("p g t -> p (g t)"),
                op=ALU.mult,
            )

        banks_taken = []
        pending = []

        def later(lag, emit):
            pending.append((len(banks_taken) - 1 + lag, emit))

        def emit_due(bank_number):
            for entry in sorted([e for e in pending if e[0] <= bank_number], key=lambda e: e[0]):
                pending.remove(entry)
                entry[1]()

        def next_bank():
            emit_due(len(banks_taken))
            tag = "bank%d" % (len(banks_taken) % BANKS)
            banks_taken.append(tag)
            bank = psum.tile([P, BANK], F32, name=tag, tag=tag)
            return bank

        def wide_stage():
            stage = work.tile([P, PASS * SLOTS], BF16, name="stage", tag="stage", bufs=4, align_bytes=64)
            return stage

        def operand(name, columns):
            codes = keep.tile([P, columns], U32, name=name + "_codes", align_bytes=64)
            scales = keep.tile([P, columns], U8, name=name + "_scales", align_bytes=64)
            return codes, scales

        def quantize(codes, scales, values):
            nc.vector.quantize_mx(out=codes.bitcast(FP8X4), scales=scales, in_=values)

        def product(out, stationary, moving, start, stop):
            nc.tensor.matmul_mx(
                out=out,
                lhsT=stationary[0].bitcast(FP8X4),
                lhsT_scale=stationary[1],
                rhs=moving[0].bitcast(FP8X4),
                rhs_scale=moving[1],
                start=start,
                stop=stop,
            )

        def columns(pair, first, count):
            return pair[0][:, first : first + count], pair[1][:, first : first + count]

        def copy_out(on_vector, out, in_):
            if on_vector:
                nc.vector.tensor_copy(out=out, in_=in_)
            else:
                nc.scalar.copy(out=out, in_=in_)

        turned, w_q, msg_q, y_t, y_scales = {}, {}, {}, {}, {}

        def turn(i):
            turned[i] = operand("turned%d" % i, PASS)
            stage = wide_stage()
            words_out = stage[:].bitcast(F32).rearrange("p (a n u) -> p a n u", a=4, u=2)
            for b in range(2):
                bank = next_bank()
                view = bank[:].rearrange("p (a u n) -> p a u n", a=2, u=2)
                for a in range(2):
                    words = turn_rows[i][2 * b + a].bitcast(F32)
                    for u in range(2):
                        nc.tensor.transpose(view[:, a, u, :], words[:, u : PASS // 2 : 2], ident[:])
                on_vector = b == 1 and i % VECTOR_TURN_EVERY == VECTOR_TURN_EVERY - 1
                copy_out(on_vector, words_out[:, 2 * b : 2 * b + 2], view.rearrange("p a u n -> p a n u"))
            later(1 if i < EDGE_GROUPS else QUANT_LAG, lambda: quantize(turned[i][0][:], turned[i][1][:], stage[:]))

        def prepare_w(g):
            w_q[g] = operand("w%d" % g, PASS)
            stages = []
            for r in range(2):
                stage = work.tile([P, 2 * P * SLOTS], BF16, name="w_stage", tag="w_stage", bufs=3, align_bytes=64)
                nc.vector.tensor_copy(
                    out=stage[:].rearrange("p (t c m j) -> p c j t m", t=2, m=2, j=SLOTS),
                    in_=w_raw[g][:].rearrange("p j (c m t) -> p c j t m", m=2, t=SLOTS)[:, :, :, 2 * r : 2 * r + 2, :],
                )
                stages.append(stage)
            for r in range(2):
                later(WLAG, lambda r=r: quantize(*columns(w_q[g], r * 2 * P, 2 * P), stages[r][:]))

        def message(g, e, r):
            quantised = operand("msg%d%d%d" % (g, e, r), 2 * P)
            for a in range(2):
                msg_q[(g, e, 2 * r + a)] = columns(quantised, a * P, P)
            act = work.tile([P, 2, 2 * P, 2], F32, name="act", tag="act", bufs=4)
            for b in range(2):
                bank = next_bank()
                for i in range(2):
                    product(
                        bank[:, i * 2 * P : (i + 1) * 2 * P],
                        columns(turned[e], (2 * b + i) * P, P),
                        columns(w_q[g], r * 2 * P, 2 * P),
                        True,
                        True,
                    )
                nc.scalar.activation(out=act[:, b], in_=bank[:].rearrange("p (i n) -> p n i", i=2), func=ACT.Tanh)
            stage = work.tile([P, 2 * P * SLOTS], BF16, name="msg_stage", tag="msg_stage", bufs=4, align_bytes=64)
            by_slot = weight[:, e : e + 1, :].rearrange("p o (b i) -> p o b i", i=2)
            later(
                READ_LAG,
                lambda: nc.vector.tensor_tensor(
                    out=stage[:].rearrange("p (n b i) -> p n b i", b=2, i=2),
                    in0=act[:].rearrange("p b n i -> p n b i"),
                    in1=by_slot.to_broadcast([P, 2 * P, 2, 2]),
                    op=ALU.mult,
                ),
            )
            later(READ_LAG + QUANT_LAG, lambda: quantize(quantised[0][:], quantised[1][:], stage[:]))

        def round_planes(g, h, n0, width):
            stage = wide_stage()
            nc.vector.tensor_copy(
                out=stage[:, : SLOTS * width].rearrange("p (c i t) -> p c t i", i=4, t=SLOTS),
                in_=y_t[(g, h)][:, :, n0 : n0 + width].rearrange("p t (c i) -> p c t i", i=4),
            )
            return stage

        def store_planes(g, first, width, stage):
            if first == 0:
                y_scales[g] = keep.tile([P, NODES], U8, name="y_scales%d" % g, align_bytes=64)
            y_codes = work.tile([P, HALF], U32, name="y_codes", tag="y_codes", bufs=3, align_bytes=64)
            quantize(y_codes[:, :width], y_scales[g][:, first : first + width], stage[:, : SLOTS * width])
            nc.sync.dma_start(
                out=out_1[g, :, first : first + width, :].rearrange("p m t -> p (m t)").bitcast(I32),
                in_=y_codes[:, :width].bitcast(I32),
            )
            if first + width == NODES:
                for quad in range(4):
                    nc.sync.dma_start(
                        out=out_2[g, 4 * quad : 4 * quad + 4, :].bitcast(I32),
                        in_=y_scales[g][32 * quad : 32 * quad + 4, :].bitcast(I32),
                    )

        def node_sum(on_vector, g, h, t, n0, width):
            if t == 0:
                y_t[(g, h)] = work.tile([P, SLOTS, HALF], F32, name="y_t", tag="y_t", bufs=3)
            bank = next_bank()
            for e in range(EDGE_GROUPS):
                nodes = columns(turned[EDGE_GROUPS * (h + 1) + e], n0, width)
                product(bank[:, :width], msg_q[(g, e, t)], nodes, e == 0, e == EDGE_GROUPS - 1)
            c = SLOTS * g + t
            factor, term = gain32[:, c : c + 1], bias_gain[:, c : c + 1]
            out = y_t[(g, h)][:, t, n0 : n0 + width]
            if on_vector:
                nc.vector.tensor_scalar(
                    out=out, in0=bank[:, :width], scalar1=factor, scalar2=term, op0=ALU.mult, op1=ALU.add
                )
            else:
                nc.scalar.activation(out=out, in_=bank[:, :width], func=ACT.Identity, bias=term, scale=factor)
            if t == SLOTS - 1:
                rounded = []
                later(READ_LAG, lambda: rounded.append(round_planes(g, h, n0, width)))
                later(READ_LAG + QUANT_LAG, lambda: store_planes(g, h * HALF + n0, width, rounded[0]))

        def store_rows(g, h, share_with_vector):
            for a in range(4):
                bank = next_bank()
                for t in range(SLOTS):
                    nc.tensor.transpose(bank[:, t * P : (t + 1) * P], y_t[(g, h)][:, t, a * P : (a + 1) * P], ident[:])
                rows = work.tile([P, PASS], F32, name="rows", tag="rows", bufs=6)
                copy_out(
                    share_with_vector and a % 2 == 1,
                    rows[:].rearrange("p (m t) -> p m t", t=SLOTS),
                    bank[:].rearrange("p (t m) -> p m t", t=SLOTS),
                )
                node0 = h * HALF + a * P
                nc.sync.dma_start(out=out_0[node0 : node0 + P, g * PASS : (g + 1) * PASS], in_=rows[:])

        last = FEATURE_GROUPS - 1
        messages = [(0, e, r) for e in range(EDGE_GROUPS) for r in range(2)]
        messages += [(g, e, r) for g in range(1, FEATURE_GROUPS) for r in range(2) for e in range(EDGE_GROUPS)]
        sums = [(g, h, t, 0, HALF) for g in range(last) for h in range(2) for t in range(SLOTS)]
        sums += [(last, h, t, 0, HALF) for h in range(2) for t in (0, 1)]
        sums += [(last, 0, t, 0, HALF) for t in (2, 3)]
        sums += [(last, 1, t, n0, QUARTER) for n0 in (0, QUARTER) for t in (2, 3)]
        out_after = {}
        for j, (g, h, t, n0, width) in enumerate(sums):
            if t == SLOTS - 1 and n0 + width == HALF:
                out_after[j + (OUT_DELAY if g < last else 2 - 2 * h)] = (g, h)

        prepare_w(0)
        for i in range(SUM_START + len(sums)):
            j = i - SUM_START
            if j == -1:
                prepare_factors()
            if j >= 0:
                node_sum(j >= VECTOR_SUMS_FROM and j % 2 == 1, *sums[j])
                if j in out_after:
                    store_rows(*out_after[j], out_after[j] == (last, 1))
            if i in turn_rows:
                turn(i)
            if 1 <= i < FEATURE_GROUPS:
                prepare_w(i)
            if 1 <= i <= len(messages):
                message(*messages[i - 1])
        emit_due(len(banks_taken) + READ_LAG + QUANT_LAG)
